import numpy as np
import ml_dtypes


def mxq(x, axis, fmt="e4m3"):
    dtype, down = {"e4m3": (ml_dtypes.float8_e4m3fn, 7), "e5m2": (ml_dtypes.float8_e5m2, 14)}[fmt]
    v = np.moveaxis(np.asarray(x, np.float32).astype(ml_dtypes.bfloat16).astype(np.float64), axis, -1)
    blocks = v.reshape(v.shape[:-1] + (-1, 32))
    amax = np.abs(blocks).max(-1, keepdims=True)
    byte = np.maximum(np.where(amax > 0, np.frexp(amax)[1] - 1 + 127, 0) - down, 1)
    scale = np.exp2(byte - 127.0)
    codes = (blocks / scale).astype(np.float32).astype(dtype).astype(np.float64)
    return np.moveaxis((codes * scale).reshape(v.shape), -1, axis)


WIDE = False


def mx_kscale(k):
    if not WIDE:
        return np.ones(k)
    levels = np.array([10, -10, 5, -5, 0])
    if k % 512:
        return np.exp2(np.random.permutation(np.resize(levels, k // 32))).repeat(32)
    a = np.empty((k // 512, 16))
    for p in range(k // 512):
        a[p, :8] = np.random.permutation(np.resize(levels, 8))
        for g in range(8):
            far = levels[np.abs(levels - a[p, g]) >= 10]
            a[p, g + 8] = far[np.random.randint(len(far))]
    return np.exp2(a.ravel()).repeat(32)


def f64(x):
    return np.asarray(x).astype(np.float64)


def striped(idx):
    return np.tile(np.asarray(idx).reshape(-1, 16).T, (8, 1)).astype(np.uint16)


def unstriped(offs):
    return offs[:16].T.reshape(-1).astype(np.int64)


def striped8(idx):
    return np.asarray(idx).reshape(8, -1, 16).transpose(0, 2, 1).reshape(128, -1).astype(np.uint16)


def unstriped8(offs):
    return offs.reshape(8, 16, -1).transpose(0, 2, 1).reshape(8, -1).astype(np.int64)


def pick8(x, idx, run):
    r = np.arange(len(x))
    return x[r[:, None], idx[r % (8 * run) // run]]


E2M1 = np.array([0.0, 0.5, 1.0, 1.5, 2.0, 3.0, 4.0, 6.0, -0.0, -0.5, -1.0, -1.5, -2.0, -3.0, -4.0, -6.0])


def pack_weight(w, fmt):
    k, n = w.shape
    w = f64(np.asarray(w, np.float32).astype(ml_dtypes.bfloat16)).reshape(k // 32, 32, n)
    amax = np.abs(w).max(1)
    if fmt == "e4m3":
        byte = np.frexp(amax)[1] - 1 + 127 - 7
    else:
        mant, ex = np.frexp(amax / 6.0)
        byte = np.where(mant > 0.5, ex, ex - 1) + 127
    byte = np.clip(np.where(amax > 0, byte, 1), 1, 254)
    scaled = (w * np.exp2(127.0 - byte)[:, None, :]).reshape(k, n).astype(np.float32)
    by_word = np.ascontiguousarray(scaled.reshape(k // 512, 128, 4, n).transpose(0, 1, 3, 2))
    if fmt == "e4m3":
        words = by_word.astype(ml_dtypes.float8_e4m3fn).view(np.uint8)
    else:
        c = by_word.astype(ml_dtypes.float4_e2m1fn).view(np.uint8) & 0xF
        words = (c[..., 0::2] | (c[..., 1::2] << 4)).reshape(k // 512, 128, 2 * n)
    return np.ascontiguousarray(words), np.ascontiguousarray(byte.astype(np.uint8).reshape(k // 512, 16, n))


def unpack_weight(words, scales, fmt):
    g, _, n = scales.shape
    words = np.ascontiguousarray(words).reshape(g, 128, n, -1)
    if fmt == "e4m3":
        vals = words.view(ml_dtypes.float8_e4m3fn).astype(np.float64)
    else:
        nib = np.empty((g, 128, n, 4), np.uint8)
        nib[..., 0::2] = words & 0xF
        nib[..., 1::2] = words >> 4
        vals = E2M1[nib]
    vals = vals * np.repeat(np.exp2(scales.astype(np.float64) - 127.0), 8, axis=1)[..., None]
    return vals.transpose(0, 1, 3, 2).reshape(g * 512, n)


def bf(x):
    return np.asarray(x, np.float32).astype(ml_dtypes.bfloat16)


def planes(Y):
    r, m = Y.shape
    b = f64(bf(Y)).reshape(r // 32, 32, m)
    amax = np.abs(b).max(1)
    byte = np.clip(np.where(amax > 0, np.frexp(amax)[1] - 1 + 127 - 7, 1), 1, 254)
    codes = (b * np.exp2(127.0 - byte)[:, None, :]).reshape(r, m).astype(np.float32).astype(ml_dtypes.float8_e4m3fn).view(np.uint8)
    words = codes.reshape(r // 512, 128, 4, m).transpose(0, 1, 3, 2)
    return np.ascontiguousarray(words), np.ascontiguousarray(byte.astype(np.uint8).reshape(r // 512, 16, m))


K, R, F, T, J, M = 512, 512, 512, 2048, 512, 256


def setup_inputs():
    n = np.random.standard_normal
    idx = np.random.permutation(T)[:J]
    idx2 = np.stack([np.random.permutation(J)[:M] for _ in range(8)])
    idx3 = np.stack([np.random.permutation(J)[:M] for _ in range(8)])
    fk = mx_kscale(K)
    fr = mx_kscale(R)
    tabp = pack_weight(n((K, T)) / fk[:, None], "e2m1")
    dtabp = pack_weight(n((K, T)) / fk[:, None], "e2m1")
    return {
        "tab_words": tabp[0],
        "tab_scales": tabp[1],
        "dtab_words": dtabp[0],
        "dtab_scales": dtabp[1],
        "w1": (n((K, R)) * 1 / np.sqrt(K) * fk[:, None]).astype(np.float32),
        "sharp": (np.random.uniform(0.1, 0.5, (1, M))).astype(np.float32),
        "rs": (np.random.uniform(0.5, 2.0, (R, 1)) * fr[:, None]).astype(np.float32),
        "wor": (n((R, F)) * 1 / np.sqrt(R) / fr[:, None]).astype(np.float32),
        "res": (n((F, M)) * 0.5).astype(np.float32),
        "offs": striped(idx),
        "offs2": striped8(idx2),
        "offs3": striped8(idx3),
    }


def reference(tab_words, tab_scales, dtab_words, dtab_scales, w1, sharp, rs, wor, res, offs, offs2, offs3):
    idx = unstriped(offs)
    idx2 = unstriped8(offs2)
    idx3 = unstriped8(offs3)
    tabu = unpack_weight(tab_words, tab_scales, "e2m1")
    dtabu = unpack_weight(dtab_words, dtab_scales, "e2m1")
    w1q = mxq(f64(w1), 0, "e4m3")
    tabidxg = tabu[:, idx]
    a = w1q.T @ tabidxg
    dtabidxg = dtabu[:, idx]
    ta = w1q.T @ dtabidxg
    dl = pick8(a, idx2, 64) - pick8(a, idx3, 64)
    u1 = np.exp(np.square(dl) * f64(sharp) * (-1.0))
    tdl = pick8(ta, idx2, 64) - pick8(ta, idx3, 64)
    tu1 = tdl * dl * 2.0 * f64(sharp) * (-1.0) * u1
    fo1 = tu1 * f64(rs)
    worq = mxq(f64(wor), 0, "e4m3")
    fo1q = mxq(fo1, 0, "e4m3")
    yo = worq.T @ fo1q
    y = yo + f64(res)
    words, scales = planes(y)
    return y, words, scales

@@ -1,0 +1,228 @@
+from contextlib import ExitStack
+
+import concourse.mybir as mybir
+from concourse.masks import make_identity
+
+K, R, F, T, J, M = 512, 512, 512, 2048, 512, 256
+FLOPS = 2 * 2 * K * R * J + 2 * R * F * M
+
+F32 = mybir.dt.float32
+BF16 = mybir.dt.bfloat16
+I32 = mybir.dt.int32
+U32 = mybir.dt.uint32
+U16 = mybir.dt.uint16
+U8 = mybir.dt.uint8
+FP8X4 = mybir.dt.float8_e4m3fn_x4
+FP4X4 = mybir.dt.float4_e2m1fn_x4
+ALU = mybir.AluOpType
+ACT = mybir.ActivationFunctionType
+
+P = 128
+PACK = 4
+HALVES = M // P
+W1_CHUNKS = 2
+WOR_CHUNKS = 2
+
+
+def tile_attend_tcpairnear_o_pl_kernel(
+    tc, tab_words, tab_scales, dtab_words, dtab_scales, w1, sharp, rs, wor, res, offs, offs2, offs3, out_0, out_1, out_2
+):
+    nc = tc.nc
+    with ExitStack() as ctx:
+        keep = ctx.enter_context(tc.tile_pool(name="keep", bufs=1))
+        shared = ctx.enter_context(tc.tile_pool(name="shared", bufs=1))
+        psum = ctx.enter_context(tc.psum_pool(name="psum", bufs=1))
+
+        def sbuf(shape, dtype, name, tag=""):
+            return keep.tile(shape, dtype, name=name, tag=tag, align_bytes=64)
+
+        def load_scale_rows(plane, rows, queue):
+            for q in range(4):
+                queue.dma_start(out=plane[32 * q : 32 * q + 4, :].bitcast(I32), in_=rows[0, 4 * q : 4 * q + 4, :].bitcast(I32))
+
+        def load_weight(w, chunks, name):
+            width = w.shape[1] // chunks
+            rows = w.rearrange("(p j) c -> p j c", j=PACK)
+            raws = []
+            for c in range(chunks):
+                raw = sbuf([P, PACK, width], F32, f"{name}_raw{c}", tag=f"raw{c}")
+                nc.sync.dma_start(out=raw[:], in_=rows[:, :, c * width : (c + 1) * width])
+                raws.append(raw)
+            return raws
+
+        def deal_and_quantise(raws, name, last_copy, at):
+            dealt = shared.tile([P, PACK, P, PACK], BF16, name=f"{name}_dealt", align_bytes=64, offset=at)
+            span = P // len(raws)
+            for c, raw in enumerate(raws):
+                copy = last_copy if c == len(raws) - 1 else nc.scalar.copy
+                copy(
+                    out=dealt[:, :, c * span : (c + 1) * span, :].rearrange("p t m j -> p m t j"),
+                    in_=raw[:].rearrange("p j (m t) -> p m t j", t=PACK),
+                )
+            codes = sbuf([P, PACK * P], U32, f"{name}_codes")
+            scales = sbuf([P, PACK * P], U8, f"{name}_scales")
+            nc.vector.quantize_mx(
+                out=codes[:].bitcast(FP8X4), scales=scales[:], in_=dealt[:].rearrange("p t m j -> p (t m j)")
+            )
+            return codes, scales
+
+        slots = keep.tile([P, J // 16], U16, name="slots")
+        left = keep.tile([P, M // 16], U16, name="left")
+        right = keep.tile([P, M // 16], U16, name="right")
+        tab_plane = sbuf([P, T], U8, "tab_plane", tag="plane_then_sharp")
+        dtab_plane = sbuf([P, T], U8, "dtab_plane", tag="plane_then_rs")
+        tab_win = sbuf([P, T], U16, "tab_win", tag="tab_then_res")
+        dtab_win = sbuf([P, T], U16, "dtab_win")
+        nc.gpsimd.memset(tab_plane[:].bitcast(I32), 0)
+        nc.vector.memset(dtab_plane[:].bitcast(I32), 0)
+
+        nc.sync.dma_start(slots[:], offs)
+        nc.sync.dma_start(left[:], offs2)
+        nc.sync.dma_start(right[:], offs3)
+        load_scale_rows(tab_plane, tab_scales, nc.scalar)
+        nc.sync.dma_start(out=tab_win[:].bitcast(I32), in_=tab_words[0].bitcast(I32))
+        w1_raws = load_weight(w1, W1_CHUNKS, "w1")
+        nc.sync.dma_start(out=dtab_win[:].bitcast(I32), in_=dtab_words[0].bitcast(I32))
+        load_scale_rows(dtab_plane, dtab_scales, nc.sync)
+
+        identity = sbuf([P, P], F32, "identity")
+        make_identity(nc, identity[:])
+
+        tab_sc = sbuf([P, J], U8, "tab_sc")
+        dtab_sc = shared.tile([P, J], U8, name="dtab_sc", align_bytes=64, offset=1024)
+        tab_cols = sbuf([P, J], U16, "tab_cols")
+        dtab_cols = shared.tile([P, J], U16, name="dtab_cols", align_bytes=64, offset=0)
+        nc.vector.tensor_copy(tab_cols[:], tab_win[:].indirect(slots[:]))
+        nc.vector.tensor_copy(tab_sc[:], tab_plane[:].indirect(slots[:]))
+        w1_codes, w1_scales = deal_and_quantise(w1_raws, "w1", nc.vector.tensor_copy, 0)
+        nc.vector.tensor_copy(dtab_cols[:], dtab_win[:].indirect(slots[:]))
+        nc.vector.tensor_copy(dtab_sc[:], dtab_plane[:].indirect(slots[:]))
+        sharp_cols = sbuf([P, HALVES], F32, "sharp_cols", tag="plane_then_sharp")
+        with nc.allow_non_contiguous_dma(reason="one sharpness to a partition"):
+            nc.sync.dma_start(out=sharp_cols[:], in_=sharp.rearrange("o (h p) -> p (o h)", p=P))
+        wor_raws = load_weight(wor, WOR_CHUNKS, "wor")
+        res_rows = sbuf([P, PACK, M], F32, "res_rows", tag="tab_then_res")
+        nc.sync.dma_start(out=res_rows[:], in_=res.rearrange("(p t) m -> p t m", t=PACK))
+
+        rs_cols = sbuf([P, PACK], F32, "rs_cols", tag="plane_then_rs")
+        nc.sync.dma_start(out=rs_cols[:], in_=rs.rearrange("(p t) o -> p (t o)", t=PACK))
+
+        def first_layer(cols, col_scales, name):
+            tiles = []
+            for t in range(PACK):
+                bank = psum.tile([P, J], F32, name=f"{name}_bank{t}", tag="product", bufs=4)
+                nc.tensor.matmul_mx(
+                    out=bank[:],
+                    lhsT=w1_codes[:, t * P : (t + 1) * P].bitcast(FP8X4),
+                    lhsT_scale=w1_scales[:, t * P : (t + 1) * P],
+                    rhs=cols[:].bitcast(FP4X4),
+                    rhs_scale=col_scales[:],
+                    start=True,
+                    stop=True,
+                )
+                whole = sbuf([P, J], F32, f"{name}{t}")
+                nc.scalar.copy(out=whole[:], in_=bank[:])
+                tiles.append(whole)
+            return tiles
+
+        a_tiles = first_layer(tab_cols, tab_sc, "a")
+        ta_tiles = first_layer(dtab_cols, dtab_sc, "ta")
+
+        neg_sharp = sbuf([P, HALVES], F32, "neg_sharp")
+        nc.scalar.activation(out=neg_sharp[:], in_=sharp_cols[:], func=ACT.Copy, scale=-1.0)
+        two_rs = sbuf([P, PACK], F32, "two_rs")
+        nc.scalar.activation(out=two_rs[:], in_=rs_cols[:], func=ACT.Copy, scale=2.0)
+
+        a_left = sbuf([P, PACK, M], F32, "a_left")
+        a_right_neg = sbuf([P, PACK, M], F32, "a_right_neg")
+        dl_banks = [psum.tile([P, R], F32, name=f"dl_bank{h}") for h in range(HALVES)]
+        for t in range(PACK):
+            nc.vector.tensor_copy(a_left[:, t, :], a_tiles[t][:].indirect(left[:]))
+            nc.vector.tensor_scalar(
+                a_right_neg[:, t, :], a_tiles[t][:].indirect(right[:]), -1.0, 0.0, ALU.mult, ALU.add
+            )
+            for h in range(HALVES):
+                pairs = slice(h * P, (h + 1) * P)
+                dst = dl_banks[h][:, t * P : (t + 1) * P]
+                nc.tensor.matmul(dst, a_left[:, t, pairs], identity[:], start=True, stop=False, is_transpose=True)
+                nc.tensor.matmul(dst, a_right_neg[:, t, pairs], identity[:], start=False, stop=True, is_transpose=True)
+
+        ta_right = sbuf([P, PACK, M], F32, "ta_right")
+        for t in range(PACK):
+            nc.vector.tensor_copy(ta_right[:, t, :], ta_tiles[t][:].indirect(right[:]))
+
+        wor_codes, wor_scales = deal_and_quantise(wor_raws, "wor", nc.scalar.copy, 4096)
+
+        gains = []
+        for h in range(HALVES):
+            squared = sbuf([P, R], F32, f"squared{h}")
+            nc.scalar.activation(out=squared[:], in_=dl_banks[h][:], func=ACT.Square)
+            u1 = sbuf([P, R], F32, f"u1_{h}", tag=f"u1_then_tdl{h}")
+            nc.scalar.activation(out=u1[:], in_=squared[:], func=ACT.Exp, scale=neg_sharp[:, h : h + 1])
+            slope = sbuf([P, R], F32, f"slope{h}")
+            nc.vector.scalar_tensor_tensor(
+                slope[:], dl_banks[h][:], neg_sharp[:, h : h + 1], u1[:], ALU.mult, ALU.mult
+            )
+            back = psum.tile([P, PACK, P], F32, name=f"back{h}")
+            for t in range(PACK):
+                nc.tensor.transpose(back[:, t, :], slope[:, t * P : (t + 1) * P], identity[:])
+            gain = sbuf([P, PACK, P], F32, f"gain{h}")
+            for t in range(PACK):
+                nc.scalar.activation(out=gain[:, t, :], in_=back[:, t, :], func=ACT.Copy, scale=two_rs[:, t : t + 1])
+            gains.append(gain)
+
+        y_words = sbuf([P, M], U32, "y_words")
+        y_scales = sbuf([P, M], U8, "y_scales")
+        out_rows = out_0.rearrange("(p t) m -> p t m", t=PACK)
+        word_rows = out_1[0].rearrange("p m t -> p (m t)").bitcast(I32)
+        for h in range(HALVES):
+            pairs = slice(h * P, (h + 1) * P)
+            entries = slice(h * P // 16, (h + 1) * P // 16)
+            tdl = sbuf([P, PACK, P], F32, f"tdl{h}", tag=f"u1_then_tdl{h}")
+            for t in range(PACK):
+                nc.vector.tensor_tensor(
+                    tdl[:, t, :], ta_tiles[t][:].indirect(left[:, entries]), ta_right[:, t, pairs], ALU.subtract
+                )
+            fo1 = sbuf([P, P, PACK], BF16, f"fo1_{h}")
+            nc.vector.tensor_tensor(
+                fo1[:].rearrange("p (c i) t -> p c t i", i=4),
+                tdl[:].rearrange("p t (c i) -> p c t i", i=4),
+                gains[h][:].rearrange("p t (c i) -> p c t i", i=4),
+                ALU.mult,
+            )
+            fo1_codes = sbuf([P, P], U32, f"fo1_codes{h}")
+            fo1_scales = sbuf([P, P], U8, f"fo1_scales{h}")
+            nc.vector.quantize_mx(
+                out=fo1_codes[:].bitcast(FP8X4), scales=fo1_scales[:], in_=fo1[:].rearrange("p m t -> p (m t)")
+            )
+            yo = psum.tile([P, PACK, P], F32, name=f"yo{h}", tag="product", bufs=4)
+            for t in range(PACK):
+                nc.tensor.matmul_mx(
+                    out=yo[:, t, :],
+                    lhsT=wor_codes[:, t * P : (t + 1) * P].bitcast(FP8X4),
+                    lhsT_scale=wor_scales[:, t * P : (t + 1) * P],
+                    rhs=fo1_codes[:].bitcast(FP8X4),
+                    rhs_scale=fo1_scales[:],
+                    start=True,
+                    stop=True,
+                )
+            y = sbuf([P, PACK, P], F32, f"y{h}")
+            nc.vector.tensor_tensor(y[:], yo[:], res_rows[:, :, pairs], ALU.add)
+            nc.sync.dma_start(out=out_rows[:, :, pairs], in_=y[:])
+            y_woven = sbuf([P, P, PACK], BF16, f"y_woven{h}")
+            weave = nc.scalar.copy if h < HALVES - 1 else nc.vector.tensor_copy
+            weave(
+                out=y_woven[:].rearrange("p (c i) t -> p c t i", i=4),
+                in_=y[:].rearrange("p t (c i) -> p c t i", i=4),
+            )
+            nc.vector.quantize_mx(
+                out=y_words[:, pairs].bitcast(FP8X4),
+                scales=y_scales[:, pairs],
+                in_=y_woven[:].rearrange("p m t -> p (m t)"),
+            )
+            nc.sync.dma_start(out=word_rows[:, pairs], in_=y_words[:, pairs].bitcast(I32))
+        for q in range(4):
+            queue = nc.scalar if q % 2 else nc.sync
+            queue.dma_start(
+                out=out_2[0, 4 * q : 4 * q + 4, :].bitcast(I32), in_=y_scales[32 * q : 32 * q + 4, :].bitcast(I32)
+            )

@@ -69,12 +69,13 @@ def tile_attend_tcpairnear_o_pl_kernel(
         slots = keep.tile([P, J // 16], U16, name="slots")
         left = keep.tile([P, M // 16], U16, name="left")
         right = keep.tile([P, M // 16], U16, name="right")
-        tab_plane = sbuf([P, T], U8, "tab_plane", tag="plane_then_sharp")
-        dtab_plane = sbuf([P, T], U8, "dtab_plane", tag="plane_then_rs")
+        tab_plane = shared.tile([P, T], U8, name="tab_plane", align_bytes=64, offset=8192)
+        dtab_plane = sbuf([P, T], U8, "dtab_plane")
         tab_win = sbuf([P, T], U16, "tab_win", tag="tab_then_res")
         dtab_win = sbuf([P, T], U16, "dtab_win")
-        nc.gpsimd.memset(tab_plane[:].bitcast(I32), 0)
-        nc.vector.memset(dtab_plane[:].bitcast(I32), 0)
+        for plane in (tab_plane, dtab_plane):
+            nc.gpsimd.memset(plane[:, : T // 2].bitcast(I32), 0)
+            nc.vector.memset(plane[:, T // 2 :].bitcast(I32), 0)
 
         nc.sync.dma_start(slots[:], offs)
         nc.sync.dma_start(left[:], offs2)
@@ -97,20 +98,19 @@ def tile_attend_tcpairnear_o_pl_kernel(
         w1_codes, w1_scales = deal_and_quantise(w1_raws, "w1", nc.vector.tensor_copy, 0)
         nc.vector.tensor_copy(dtab_cols[:], dtab_win[:].indirect(slots[:]))
         nc.vector.tensor_copy(dtab_sc[:], dtab_plane[:].indirect(slots[:]))
-        sharp_cols = sbuf([P, HALVES], F32, "sharp_cols", tag="plane_then_sharp")
+        rs_cols = shared.tile([P, PACK], F32, name="rs_cols", align_bytes=64, offset=8192 + 64)
+        nc.sync.dma_start(out=rs_cols[:], in_=rs.rearrange("(p t) o -> p (t o)", t=PACK))
+        sharp_cols = shared.tile([P, HALVES], F32, name="sharp_cols", align_bytes=64, offset=8192)
         with nc.allow_non_contiguous_dma(reason="one sharpness to a partition"):
             nc.sync.dma_start(out=sharp_cols[:], in_=sharp.rearrange("o (h p) -> p (o h)", p=P))
         wor_raws = load_weight(wor, WOR_CHUNKS, "wor")
         res_rows = sbuf([P, PACK, M], F32, "res_rows", tag="tab_then_res")
         nc.sync.dma_start(out=res_rows[:], in_=res.rearrange("(p t) m -> p t m", t=PACK))
 
-        rs_cols = sbuf([P, PACK], F32, "rs_cols", tag="plane_then_rs")
-        nc.sync.dma_start(out=rs_cols[:], in_=rs.rearrange("(p t) o -> p (t o)", t=PACK))
-
         def first_layer(cols, col_scales, name):
             tiles = []
             for t in range(PACK):
-                bank = psum.tile([P, J], F32, name=f"{name}_bank{t}", tag="product", bufs=4)
+                bank = psum.tile([P, J], F32, name=f"{name}_bank{t}", tag="product", bufs=2)
                 nc.tensor.matmul_mx(
                     out=bank[:],
                     lhsT=w1_codes[:, t * P : (t + 1) * P].bitcast(FP8X4),
@@ -128,48 +128,79 @@ def tile_attend_tcpairnear_o_pl_kernel(
         a_tiles = first_layer(tab_cols, tab_sc, "a")
         ta_tiles = first_layer(dtab_cols, dtab_sc, "ta")
 
-        neg_sharp = sbuf([P, HALVES], F32, "neg_sharp")
-        nc.scalar.activation(out=neg_sharp[:], in_=sharp_cols[:], func=ACT.Copy, scale=-1.0)
-        two_rs = sbuf([P, PACK], F32, "two_rs")
-        nc.scalar.activation(out=two_rs[:], in_=rs_cols[:], func=ACT.Copy, scale=2.0)
-
-        a_left = sbuf([P, PACK, M], F32, "a_left")
-        a_right_neg = sbuf([P, PACK, M], F32, "a_right_neg")
-        dl_banks = [psum.tile([P, R], F32, name=f"dl_bank{h}") for h in range(HALVES)]
-        for t in range(PACK):
-            nc.vector.tensor_copy(a_left[:, t, :], a_tiles[t][:].indirect(left[:]))
-            nc.vector.tensor_scalar(
-                a_right_neg[:, t, :], a_tiles[t][:].indirect(right[:]), -1.0, 0.0, ALU.mult, ALU.add
-            )
+        def turn_and_add(banks, pair, t):
             for h in range(HALVES):
                 pairs = slice(h * P, (h + 1) * P)
-                dst = dl_banks[h][:, t * P : (t + 1) * P]
-                nc.tensor.matmul(dst, a_left[:, t, pairs], identity[:], start=True, stop=False, is_transpose=True)
-                nc.tensor.matmul(dst, a_right_neg[:, t, pairs], identity[:], start=False, stop=True, is_transpose=True)
+                dst = banks[h][:, t * P : (t + 1) * P]
+                nc.tensor.matmul(dst, pair[:, 0, pairs], identity[:], start=True, stop=False, is_transpose=True)
+                nc.tensor.matmul(dst, pair[:, 1, pairs], identity[:], start=False, stop=True, is_transpose=True)
 
-        ta_right = sbuf([P, PACK, M], F32, "ta_right")
+        def look_up_pair(window, name):
+            pair = sbuf([P, 2, M], F32, name)
+            nc.vector.tensor_copy(pair[:, 0, :], window[:].indirect(left[:]))
+            nc.vector.tensor_scalar(pair[:, 1, :], window[:].indirect(right[:]), -1.0, 0.0, ALU.mult, ALU.add)
+            return pair
+
+        dl_banks = [psum.tile([P, R], F32, name=f"dl_bank{h}", tag=f"dl_then_back{h}") for h in range(HALVES)]
+        scaled_banks = [psum.tile([P, R], F32, name=f"scaled_bank{h}") for h in range(HALVES)]
+        tdl_banks = [psum.tile([P, R], F32, name=f"tdl_bank{h}") for h in range(HALVES)]
         for t in range(PACK):
-            nc.vector.tensor_copy(ta_right[:, t, :], ta_tiles[t][:].indirect(right[:]))
+            pair = look_up_pair(a_tiles[t], f"a_pair{t}")
+            turn_and_add(dl_banks, pair, t)
+            scaled = sbuf([P, 2, M], F32, f"a_scaled{t}")
+            nc.scalar.activation(out=scaled[:], in_=pair[:], func=ACT.Copy, scale=rs_cols[:, t : t + 1])
+            turn_and_add(scaled_banks, scaled, t)
+        for t in range(PACK):
+            turn_and_add(tdl_banks, look_up_pair(ta_tiles[t], f"ta_pair{t}"), t)
+
+        neg_sharp = sbuf([P, HALVES], F32, "neg_sharp")
+        nc.scalar.activation(out=neg_sharp[:], in_=sharp_cols[:], func=ACT.Copy, scale=-1.0)
+        neg_two_sharp = sbuf([P, HALVES], F32, "neg_two_sharp")
+        nc.scalar.activation(out=neg_two_sharp[:], in_=sharp_cols[:], func=ACT.Copy, scale=-2.0)
+
+        slopes = []
+        for h in range(HALVES):
+            squared = sbuf([P, R], F32, f"squared{h}")
+            nc.scalar.activation(
+                out=squared[:].rearrange("m (u p e) -> m u p e", u=2, e=2),
+                in_=dl_banks[h][:].rearrange("m (u e p) -> m u p e", u=2, e=2),
+                func=ACT.Square,
+            )
+            u1 = sbuf([P, R], F32, f"u1_{h}")
+            nc.scalar.activation(out=u1[:], in_=squared[:], func=ACT.Exp, scale=neg_sharp[:, h : h + 1])
+            slope = sbuf([P, R], F32, f"slope{h}")
+            for u in range(2):
+                run = slice(u * 2 * P, (u + 1) * 2 * P)
+                nc.vector.scalar_tensor_tensor(
+                    slope[:, run].rearrange("m (p e) -> m p e", e=2),
+                    scaled_banks[h][:, run].rearrange("m (e p) -> m p e", e=2),
+                    neg_two_sharp[:, h : h + 1],
+                    u1[:, run].rearrange("m (p e) -> m p e", e=2),
+                    ALU.mult,
+                    ALU.mult,
+                )
+            slopes.append(slope)
 
         wor_codes, wor_scales = deal_and_quantise(wor_raws, "wor", nc.scalar.copy, 4096)
 
-        gains = []
+        fo1s = []
         for h in range(HALVES):
-            squared = sbuf([P, R], F32, f"squared{h}")
-            nc.scalar.activation(out=squared[:], in_=dl_banks[h][:], func=ACT.Square)
-            u1 = sbuf([P, R], F32, f"u1_{h}", tag=f"u1_then_tdl{h}")
-            nc.scalar.activation(out=u1[:], in_=squared[:], func=ACT.Exp, scale=neg_sharp[:, h : h + 1])
-            slope = sbuf([P, R], F32, f"slope{h}")
-            nc.vector.scalar_tensor_tensor(
-                slope[:], dl_banks[h][:], neg_sharp[:, h : h + 1], u1[:], ALU.mult, ALU.mult
+            fo1_turned = sbuf([P, 2, P, 2], BF16, f"fo1_turned{h}")
+            nc.vector.tensor_tensor(
+                fo1_turned[:],
+                tdl_banks[h][:].rearrange("m (u e p) -> m u p e", u=2, e=2),
+                slopes[h][:].rearrange("m (u p e) -> m u p e", u=2, e=2),
+                ALU.mult,
             )
-            back = psum.tile([P, PACK, P], F32, name=f"back{h}")
-            for t in range(PACK):
-                nc.tensor.transpose(back[:, t, :], slope[:, t * P : (t + 1) * P], identity[:])
-            gain = sbuf([P, PACK, P], F32, f"gain{h}")
-            for t in range(PACK):
-                nc.scalar.activation(out=gain[:, t, :], in_=back[:, t, :], func=ACT.Copy, scale=two_rs[:, t : t + 1])
-            gains.append(gain)
+            words = fo1_turned[:].rearrange("m u p e -> m (u p e)").bitcast(F32)
+            back = psum.tile([P, 2, P], F32, name=f"back{h}", tag=f"dl_then_back{h}")
+            for u in range(2):
+                nc.tensor.transpose(back[:, u, :], words[:, u * P : (u + 1) * P], identity[:])
+            fo1 = sbuf([P, P * PACK], BF16, f"fo1_{h}")
+            nc.scalar.copy(
+                out=fo1[:].bitcast(F32).rearrange("p (m u) -> p m u", u=2), in_=back[:].rearrange("p u m -> p m u")
+            )
+            fo1s.append(fo1)
 
         y_words = sbuf([P, M], U32, "y_words")
         y_scales = sbuf([P, M], U8, "y_scales")
@@ -177,25 +208,12 @@ def tile_attend_tcpairnear_o_pl_kernel(
         word_rows = out_1[0].rearrange("p m t -> p (m t)").bitcast(I32)
         for h in range(HALVES):
             pairs = slice(h * P, (h + 1) * P)
-            entries = slice(h * P // 16, (h + 1) * P // 16)
-            tdl = sbuf([P, PACK, P], F32, f"tdl{h}", tag=f"u1_then_tdl{h}")
-            for t in range(PACK):
-                nc.vector.tensor_tensor(
-                    tdl[:, t, :], ta_tiles[t][:].indirect(left[:, entries]), ta_right[:, t, pairs], ALU.subtract
-                )
-            fo1 = sbuf([P, P, PACK], BF16, f"fo1_{h}")
-            nc.vector.tensor_tensor(
-                fo1[:].rearrange("p (c i) t -> p c t i", i=4),
-                tdl[:].rearrange("p t (c i) -> p c t i", i=4),
-                gains[h][:].rearrange("p t (c i) -> p c t i", i=4),
-                ALU.mult,
-            )
             fo1_codes = sbuf([P, P], U32, f"fo1_codes{h}")
             fo1_scales = sbuf([P, P], U8, f"fo1_scales{h}")
             nc.vector.quantize_mx(
-                out=fo1_codes[:].bitcast(FP8X4), scales=fo1_scales[:], in_=fo1[:].rearrange("p m t -> p (m t)")
+                out=fo1_codes[:].bitcast(FP8X4), scales=fo1_scales[:], in_=fo1s[h][:]
             )
-            yo = psum.tile([P, PACK, P], F32, name=f"yo{h}", tag="product", bufs=4)
+            yo = psum.tile([P, PACK, P], F32, name=f"yo{h}", tag="product", bufs=2)
             for t in range(PACK):
                 nc.tensor.matmul_mx(
                     out=yo[:, t, :],

from contextlib import ExitStack

import concourse.mybir as mybir
from concourse.masks import make_identity

K, R, F, T, J, M = 512, 512, 512, 2048, 512, 256
FLOPS = 2 * 2 * K * R * J + 2 * R * F * M

F32 = mybir.dt.float32
BF16 = mybir.dt.bfloat16
I32 = mybir.dt.int32
U32 = mybir.dt.uint32
U16 = mybir.dt.uint16
U8 = mybir.dt.uint8
FP8X4 = mybir.dt.float8_e4m3fn_x4
FP4X4 = mybir.dt.float4_e2m1fn_x4
ALU = mybir.AluOpType
ACT = mybir.ActivationFunctionType

P = 128
PACK = 4
HALVES = M // P
W1_CHUNKS = 2
WOR_CHUNKS = 2


def tile_attend_tcpairnear_o_pl_kernel(
    tc, tab_words, tab_scales, dtab_words, dtab_scales, w1, sharp, rs, wor, res, offs, offs2, offs3, out_0, out_1, out_2
):
    nc = tc.nc
    with ExitStack() as ctx:
        keep = ctx.enter_context(tc.tile_pool(name="keep", bufs=1))
        shared = ctx.enter_context(tc.tile_pool(name="shared", bufs=1))
        psum = ctx.enter_context(tc.psum_pool(name="psum", bufs=1))

        def sbuf(shape, dtype, name, tag=""):
            return keep.tile(shape, dtype, name=name, tag=tag, align_bytes=64)

        def load_scale_rows(plane, rows, queue):
            for q in range(4):
                queue.dma_start(out=plane[32 * q : 32 * q + 4, :].bitcast(I32), in_=rows[0, 4 * q : 4 * q + 4, :].bitcast(I32))

        def load_weight(w, chunks, name):
            width = w.shape[1] // chunks
            rows = w.rearrange("(p j) c -> p j c", j=PACK)
            raws = []
            for c in range(chunks):
                raw = sbuf([P, PACK, width], F32, f"{name}_raw{c}", tag=f"raw{c}")
                nc.sync.dma_start(out=raw[:], in_=rows[:, :, c * width : (c + 1) * width])
                raws.append(raw)
            return raws

        def deal_and_quantise(raws, name, last_copy, at):
            dealt = shared.tile([P, PACK, P, PACK], BF16, name=f"{name}_dealt", align_bytes=64, offset=at)
            span = P // len(raws)
            for c, raw in enumerate(raws):
                copy = last_copy if c == len(raws) - 1 else nc.scalar.copy
                copy(
                    out=dealt[:, :, c * span : (c + 1) * span, :].rearrange("p t m j -> p m t j"),
                    in_=raw[:].rearrange("p j (m t) -> p m t j", t=PACK),
                )
            codes = sbuf([P, PACK * P], U32, f"{name}_codes")
            scales = sbuf([P, PACK * P], U8, f"{name}_scales")
            nc.vector.quantize_mx(
                out=codes[:].bitcast(FP8X4), scales=scales[:], in_=dealt[:].rearrange("p t m j -> p (t m j)")
            )
            return codes, scales

        slots = keep.tile([P, J // 16], U16, name="slots")
        left = keep.tile([P, M // 16], U16, name="left")
        right = keep.tile([P, M // 16], U16, name="right")
        tab_plane = shared.tile([P, T], U8, name="tab_plane", align_bytes=64, offset=8192)
        dtab_plane = sbuf([P, T], U8, "dtab_plane")
        tab_win = sbuf([P, T], U16, "tab_win", tag="tab_then_res")
        dtab_win = sbuf([P, T], U16, "dtab_win")
        for plane in (tab_plane, dtab_plane):
            nc.gpsimd.memset(plane[:, : T // 2].bitcast(I32), 0)
            nc.vector.memset(plane[:, T // 2 :].bitcast(I32), 0)

        nc.sync.dma_start(slots[:], offs)
        nc.sync.dma_start(left[:], offs2)
        nc.sync.dma_start(right[:], offs3)
        load_scale_rows(tab_plane, tab_scales, nc.scalar)
        nc.sync.dma_start(out=tab_win[:].bitcast(I32), in_=tab_words[0].bitcast(I32))
        w1_raws = load_weight(w1, W1_CHUNKS, "w1")
        nc.sync.dma_start(out=dtab_win[:].bitcast(I32), in_=dtab_words[0].bitcast(I32))
        load_scale_rows(dtab_plane, dtab_scales, nc.sync)

        identity = sbuf([P, P], F32, "identity")
        make_identity(nc, identity[:])

        tab_sc = sbuf([P, J], U8, "tab_sc")
        dtab_sc = shared.tile([P, J], U8, name="dtab_sc", align_bytes=64, offset=1024)
        tab_cols = sbuf([P, J], U16, "tab_cols")
        dtab_cols = shared.tile([P, J], U16, name="dtab_cols", align_bytes=64, offset=0)
        nc.vector.tensor_copy(tab_cols[:], tab_win[:].indirect(slots[:]))
        nc.vector.tensor_copy(tab_sc[:], tab_plane[:].indirect(slots[:]))
        w1_codes, w1_scales = deal_and_quantise(w1_raws, "w1", nc.vector.tensor_copy, 0)
        nc.vector.tensor_copy(dtab_cols[:], dtab_win[:].indirect(slots[:]))
        nc.vector.tensor_copy(dtab_sc[:], dtab_plane[:].indirect(slots[:]))
        rs_cols = shared.tile([P, PACK], F32, name="rs_cols", align_bytes=64, offset=8192 + 64)
        nc.sync.dma_start(out=rs_cols[:], in_=rs.rearrange("(p t) o -> p (t o)", t=PACK))
        sharp_cols = shared.tile([P, HALVES], F32, name="sharp_cols", align_bytes=64, offset=8192)
        with nc.allow_non_contiguous_dma(reason="one sharpness to a partition"):
            nc.sync.dma_start(out=sharp_cols[:], in_=sharp.rearrange("o (h p) -> p (o h)", p=P))
        wor_raws = load_weight(wor, WOR_CHUNKS, "wor")
        res_rows = sbuf([P, PACK, M], F32, "res_rows", tag="tab_then_res")
        nc.sync.dma_start(out=res_rows[:], in_=res.rearrange("(p t) m -> p t m", t=PACK))

        def first_layer(cols, col_scales, name):
            tiles = []
            for t in range(PACK):
                bank = psum.tile([P, J], F32, name=f"{name}_bank{t}", tag="product", bufs=2)
                nc.tensor.matmul_mx(
                    out=bank[:],
                    lhsT=w1_codes[:, t * P : (t + 1) * P].bitcast(FP8X4),
                    lhsT_scale=w1_scales[:, t * P : (t + 1) * P],
                    rhs=cols[:].bitcast(FP4X4),
                    rhs_scale=col_scales[:],
                    start=True,
                    stop=True,
                )
                whole = sbuf([P, J], F32, f"{name}{t}")
                nc.scalar.copy(out=whole[:], in_=bank[:])
                tiles.append(whole)
            return tiles

        a_tiles = first_layer(tab_cols, tab_sc, "a")
        ta_tiles = first_layer(dtab_cols, dtab_sc, "ta")

        def turn_and_add(banks, pair, t):
            for h in range(HALVES):
                pairs = slice(h * P, (h + 1) * P)
                dst = banks[h][:, t * P : (t + 1) * P]
                nc.tensor.matmul(dst, pair[:, 0, pairs], identity[:], start=True, stop=False, is_transpose=True)
                nc.tensor.matmul(dst, pair[:, 1, pairs], identity[:], start=False, stop=True, is_transpose=True)

        def look_up_pair(window, name):
            pair = sbuf([P, 2, M], F32, name)
            nc.vector.tensor_copy(pair[:, 0, :], window[:].indirect(left[:]))
            nc.vector.tensor_scalar(pair[:, 1, :], window[:].indirect(right[:]), -1.0, 0.0, ALU.mult, ALU.add)
            return pair

        dl_banks = [psum.tile([P, R], F32, name=f"dl_bank{h}", tag=f"dl_then_back{h}") for h in range(HALVES)]
        scaled_banks = [psum.tile([P, R], F32, name=f"scaled_bank{h}") for h in range(HALVES)]
        tdl_banks = [psum.tile([P, R], F32, name=f"tdl_bank{h}") for h in range(HALVES)]
        for t in range(PACK):
            pair = look_up_pair(a_tiles[t], f"a_pair{t}")
            turn_and_add(dl_banks, pair, t)
            scaled = sbuf([P, 2, M], F32, f"a_scaled{t}")
            nc.scalar.activation(out=scaled[:], in_=pair[:], func=ACT.Copy, scale=rs_cols[:, t : t + 1])
            turn_and_add(scaled_banks, scaled, t)
        for t in range(PACK):
            turn_and_add(tdl_banks, look_up_pair(ta_tiles[t], f"ta_pair{t}"), t)

        neg_sharp = sbuf([P, HALVES], F32, "neg_sharp")
        nc.scalar.activation(out=neg_sharp[:], in_=sharp_cols[:], func=ACT.Copy, scale=-1.0)
        neg_two_sharp = sbuf([P, HALVES], F32, "neg_two_sharp")
        nc.scalar.activation(out=neg_two_sharp[:], in_=sharp_cols[:], func=ACT.Copy, scale=-2.0)

        slopes = []
        for h in range(HALVES):
            squared = sbuf([P, R], F32, f"squared{h}")
            nc.scalar.activation(
                out=squared[:].rearrange("m (u p e) -> m u p e", u=2, e=2),
                in_=dl_banks[h][:].rearrange("m (u e p) -> m u p e", u=2, e=2),
                func=ACT.Square,
            )
            u1 = sbuf([P, R], F32, f"u1_{h}")
            nc.scalar.activation(out=u1[:], in_=squared[:], func=ACT.Exp, scale=neg_sharp[:, h : h + 1])
            slope = sbuf([P, R], F32, f"slope{h}")
            for u in range(2):
                run = slice(u * 2 * P, (u + 1) * 2 * P)
                nc.vector.scalar_tensor_tensor(
                    slope[:, run].rearrange("m (p e) -> m p e", e=2),
                    scaled_banks[h][:, run].rearrange("m (e p) -> m p e", e=2),
                    neg_two_sharp[:, h : h + 1],
                    u1[:, run].rearrange("m (p e) -> m p e", e=2),
                    ALU.mult,
                    ALU.mult,
                )
            slopes.append(slope)

        wor_codes, wor_scales = deal_and_quantise(wor_raws, "wor", nc.scalar.copy, 4096)

        fo1s = []
        for h in range(HALVES):
            fo1_turned = sbuf([P, 2, P, 2], BF16, f"fo1_turned{h}")
            nc.vector.tensor_tensor(
                fo1_turned[:],
                tdl_banks[h][:].rearrange("m (u e p) -> m u p e", u=2, e=2),
                slopes[h][:].rearrange("m (u p e) -> m u p e", u=2, e=2),
                ALU.mult,
            )
            words = fo1_turned[:].rearrange("m u p e -> m (u p e)").bitcast(F32)
            back = psum.tile([P, 2, P], F32, name=f"back{h}", tag=f"dl_then_back{h}")
            for u in range(2):
                nc.tensor.transpose(back[:, u, :], words[:, u * P : (u + 1) * P], identity[:])
            fo1 = sbuf([P, P * PACK], BF16, f"fo1_{h}")
            nc.scalar.copy(
                out=fo1[:].bitcast(F32).rearrange("p (m u) -> p m u", u=2), in_=back[:].rearrange("p u m -> p m u")
            )
            fo1s.append(fo1)

        y_words = sbuf([P, M], U32, "y_words")
        y_scales = sbuf([P, M], U8, "y_scales")
        out_rows = out_0.rearrange("(p t) m -> p t m", t=PACK)
        word_rows = out_1[0].rearrange("p m t -> p (m t)").bitcast(I32)
        for h in range(HALVES):
            pairs = slice(h * P, (h + 1) * P)
            fo1_codes = sbuf([P, P], U32, f"fo1_codes{h}")
            fo1_scales = sbuf([P, P], U8, f"fo1_scales{h}")
            nc.vector.quantize_mx(
                out=fo1_codes[:].bitcast(FP8X4), scales=fo1_scales[:], in_=fo1s[h][:]
            )
            yo = psum.tile([P, PACK, P], F32, name=f"yo{h}", tag="product", bufs=2)
            for t in range(PACK):
                nc.tensor.matmul_mx(
                    out=yo[:, t, :],
                    lhsT=wor_codes[:, t * P : (t + 1) * P].bitcast(FP8X4),
                    lhsT_scale=wor_scales[:, t * P : (t + 1) * P],
                    rhs=fo1_codes[:].bitcast(FP8X4),
                    rhs_scale=fo1_scales[:],
                    start=True,
                    stop=True,
                )
            y = sbuf([P, PACK, P], F32, f"y{h}")
            nc.vector.tensor_tensor(y[:], yo[:], res_rows[:, :, pairs], ALU.add)
            nc.sync.dma_start(out=out_rows[:, :, pairs], in_=y[:])
            y_woven = sbuf([P, P, PACK], BF16, f"y_woven{h}")
            weave = nc.scalar.copy if h < HALVES - 1 else nc.vector.tensor_copy
            weave(
                out=y_woven[:].rearrange("p (c i) t -> p c t i", i=4),
                in_=y[:].rearrange("p t (c i) -> p c t i", i=4),
            )
            nc.vector.quantize_mx(
                out=y_words[:, pairs].bitcast(FP8X4),
                scales=y_scales[:, pairs],
                in_=y_woven[:].rearrange("p m t -> p (m t)"),
            )
            nc.sync.dma_start(out=word_rows[:, pairs], in_=y_words[:, pairs].bitcast(I32))
        for q in range(4):
            queue = nc.scalar if q % 2 else nc.sync
            queue.dma_start(
                out=out_2[0, 4 * q : 4 * q + 4, :].bitcast(I32), in_=y_scales[32 * q : 32 * q + 4, :].bitcast(I32)
            )
